import numpy as np
import ml_dtypes


def mxq(x, axis, fmt="e4m3"):
    dtype, down = {"e4m3": (ml_dtypes.float8_e4m3fn, 7), "e5m2": (ml_dtypes.float8_e5m2, 14)}[fmt]
    v = np.moveaxis(np.asarray(x, np.float32).astype(ml_dtypes.bfloat16).astype(np.float64), axis, -1)
    blocks = v.reshape(v.shape[:-1] + (-1, 32))
    amax = np.abs(blocks).max(-1, keepdims=True)
    byte = np.maximum(np.where(amax > 0, np.frexp(amax)[1] - 1 + 127, 0) - down, 1)
    scale = np.exp2(byte - 127.0)
    codes = (blocks / scale).astype(np.float32).astype(dtype).astype(np.float64)
    return np.moveaxis((codes * scale).reshape(v.shape), -1, axis)


WIDE = False


def mx_kscale(k):
    if not WIDE:
        return np.ones(k)
    levels = np.array([30, -30])
    if k % 512:
        return np.exp2(np.random.permutation(np.resize(levels, k // 32))).repeat(32)
    a = np.empty((k // 512, 16))
    for p in range(k // 512):
        a[p, :8] = np.random.permutation(np.resize(levels, 8))
        for g in range(8):
            far = levels[np.abs(levels - a[p, g]) >= 10]
            a[p, g + 8] = far[np.random.randint(len(far))]
    return np.exp2(a.ravel()).repeat(32)


def f64(x):
    return np.asarray(x).astype(np.float64)


def striped(idx):
    return np.tile(np.asarray(idx).reshape(-1, 16).T, (8, 1)).astype(np.uint16)


def unstriped(offs):
    return offs[:16].T.reshape(-1).astype(np.int64)


K, J, N, T, B, V, Q = 256, 1024, 256, 2048, 128, 2048, 1024


def setup_inputs():
    n = np.random.standard_normal
    idx = np.random.permutation(T)[:J]
    idx2 = np.random.permutation(V)[:J]
    idx3 = np.random.permutation(Q)[:N]
    fj = mx_kscale(J)
    return {
        "xf": (n((K, T))).astype(np.float32),
        "ra": (np.random.uniform(0.5, 1.5, (1, J)) * fj).astype(np.float32),
        "gt": (n((N, V)) * np.exp(0.5 * n((1, V)))).astype(np.float32),
        "rb": (np.random.uniform(0.5, 1.5, (1, J)) / fj).astype(np.float32),
        "sv": (n((N, V))).astype(np.float32),
        "old": (0.5 * n((K, Q))).astype(np.float32),
        "offs": striped(idx),
        "offs2": striped(idx2),
        "offs3": striped(idx3),
    }


def reference(xf, ra, gt, rb, sv, old, offs, offs2, offs3):
    idx = unstriped(offs)
    idx2 = unstriped(offs2)
    idx3 = unstriped(offs3)
    xg = f64(xf)[:, idx]
    g1 = xg.reshape(K, B, J // B).mean(axis=2)
    g2 = np.repeat(g1, J // B, axis=1)
    us = (xg - g2) * f64(ra)
    uj = us.T
    gs = f64(gt)[:, idx2] * np.maximum(f64(sv)[:, idx2], 0.0) * f64(rb)
    gj = gs.T
    ujq = mxq(uj, 0, "e4m3")
    gjq = mxq(gj, 0, "e5m2")
    w = ujq.T @ gjq
    wp = np.zeros((K, Q))
    wp[:, idx3] = w
    y = 0.04 * wp + f64(old)
    return y

@@ -1,0 +1,199 @@
+from contextlib import ExitStack
+
+import concourse.mybir as mybir
+from concourse.masks import make_identity
+
+K, J, N, T, V, Q = 256, 1024, 256, 2048, 2048, 1024
+FLOPS = 2 * K * N * J
+
+F32 = mybir.dt.float32
+BF16 = mybir.dt.bfloat16
+U32 = mybir.dt.uint32
+U16 = mybir.dt.uint16
+U8 = mybir.dt.uint8
+E4M3 = mybir.dt.float8_e4m3fn_x4
+E5M2 = mybir.dt.float8_e5m2_x4
+ALU = mybir.AluOpType
+COPY = mybir.ActivationFunctionType.Copy
+
+P = 128
+PACK = 4
+PASS = P * PACK
+PASSES = J // PASS
+GROUP = 8
+LIST_ROWS = 16
+STEP = 0.04
+LOADS = "xl x0 x1 ra gl s0 g0 s1 rb g1 wl o0 o1"
+XV = [[512,0],[512,0]]
+SV = [[0,0],[256,0]]
+GV = [[0,0],[256,0]]
+
+
+def tile_list_moment_centred_saved_placed_kernel(tc, xf, ra, gt, rb, sv, old, offs, offs2, offs3, out):
+    nc = tc.nc
+    with ExitStack() as ctx:
+        lists = ctx.enter_context(tc.tile_pool(name="lists", bufs=1))
+        sb = ctx.enter_context(tc.tile_pool(name="sb", bufs=1))
+        turn = ctx.enter_context(tc.psum_pool(name="turn", bufs=6))
+        sums = ctx.enter_context(tc.psum_pool(name="sums", bufs=1))
+
+        x_list = lists.tile([P, J // LIST_ROWS], U16, name="x_list")
+        g_list = lists.tile([P, J // LIST_ROWS], U16, name="g_list")
+        w_list = lists.tile([P, N // LIST_ROWS], U16, name="w_list")
+        ra_sb = sb.tile([P, PASSES, PACK], F32, name="ra_sb")
+        rb_sb = sb.tile([P, PASSES, PACK], F32, name="rb_sb")
+        x_tab = [sb.tile([P, T], F32, name=f"x_tab{h}") for h in range(2)]
+        s_tab = [sb.tile([P, V], F32, name=f"s_tab{h}") for h in range(2)]
+        g_tab = [sb.tile([P, V], F32, name=f"g_tab{h}") for h in range(2)]
+        old_sb = [sb.tile([P, Q], F32, name=f"old_sb{h}") for h in range(2)]
+        placed = [sb.tile([P, Q], F32, name=f"placed{h}") for h in range(2)]
+        ident = sb.tile([P, P], F32, name="ident")
+
+        def rows(h):
+            return slice(h * P, (h + 1) * P)
+
+        loads = {
+            "xl": (x_list[:], offs), "gl": (g_list[:], offs2), "wl": (w_list[:], offs3),
+            "x0": (x_tab[0][:], xf[rows(0), :]), "x1": (x_tab[1][:], xf[rows(1), :]),
+            "s0": (s_tab[0][:], sv[rows(0), :]), "s1": (s_tab[1][:], sv[rows(1), :]),
+            "g0": (g_tab[0][:], gt[rows(0), :]), "g1": (g_tab[1][:], gt[rows(1), :]),
+            "o0": (old_sb[0][:], old[rows(0), :]), "o1": (old_sb[1][:], old[rows(1), :]),
+            "ra": (ra_sb[:], ra.rearrange("o (g p t) -> p (o g) t", p=P, t=PACK)),
+            "rb": (rb_sb[:], rb.rearrange("o (g p t) -> p (o g) t", p=P, t=PACK)),
+        }
+        for name in LOADS.split():
+            nc.sync.dma_start(*loads[name])
+
+        make_identity(nc, ident[:])
+        for h in range(2):
+            nc.gpsimd.memset(placed[h][:], 0.0)
+
+        def gather(on_vector, name, table, offsets, g):
+            picked = sb.tile([P, PASS], F32, name=name)
+            for lo, hi in ((0, on_vector), (on_vector, PASS)):
+                if hi == lo:
+                    continue
+                src = table[:].indirect(offsets[:, (g * PASS + lo) // LIST_ROWS : (g * PASS + hi) // LIST_ROWS])
+                if hi == on_vector:
+                    nc.vector.tensor_copy(picked[:, lo:hi], src)
+                else:
+                    nc.scalar.activation(picked[:, lo:hi], src, COPY)
+            return picked
+
+        u_codes, u_scales = {}, {}
+        groups = PASS // GROUP
+
+        def features(h):
+            u_bf = sb.tile([P, PASSES * PASS], BF16, name=f"u_bf{h}", align_bytes=64)
+            picked = [gather(XV[h][g], f"xg{h}{g}", x_tab[h], x_list, g) for g in range(PASSES)]
+            for g in range(PASSES):
+                xg = picked[g]
+                total = sb.tile([P, groups], F32, name=f"total{h}{g}")
+                nc.vector.tensor_reduce(
+                    total[:], xg[:].rearrange("k (b i) -> k b i", i=GROUP), mybir.AxisListType.X, ALU.add
+                )
+                neg_mean = sb.tile([P, P], F32, name=f"neg_mean{h}{g}")
+                nc.vector.tensor_scalar_mul(
+                    neg_mean[:].rearrange("k (b e) -> k b e", e=2),
+                    total[:].unsqueeze(2).to_broadcast([P, groups, 2]),
+                    -1.0 / GROUP,
+                )
+                bank = turn.tile([P, PACK, P], F32, name="bank")
+                for t in range(PACK):
+                    nc.tensor.matmul(bank[:, t, :], xg[:, t:PASS:PACK], ident[:], start=(t == 0), stop=False, is_transpose=True)
+                for t in range(PACK):
+                    nc.tensor.matmul(bank[:, t, :], neg_mean[:], ident[:], start=False, stop=(t == PACK - 1), is_transpose=True)
+                nc.vector.tensor_tensor(
+                    u_bf[:, g * PASS : (g + 1) * PASS].rearrange("p (c t) -> p c t", t=PACK),
+                    bank[:].rearrange("p t c -> p c t"),
+                    ra_sb[:, g, :].unsqueeze(1).to_broadcast([P, P, PACK]),
+                    ALU.mult,
+                )
+            codes = sb.tile([P, PASSES * P], U32, name=f"u_codes{h}", align_bytes=64)
+            scales = sb.tile([P, PASSES * P], U8, name=f"u_scales{h}", align_bytes=64)
+            nc.vector.quantize_mx(codes[:].bitcast(E4M3), scales[:], u_bf[:])
+            u_codes[h] = codes
+            u_scales[h] = scales
+
+        def product(acc, h, g, codes, scales):
+            nc.tensor.matmul_mx(
+                acc,
+                lhsT=u_codes[h][:, g * P : (g + 1) * P].bitcast(E4M3),
+                lhsT_scale=u_scales[h][:, g * P : (g + 1) * P],
+                rhs=codes[:].bitcast(E5M2),
+                rhs_scale=scales[:],
+                start=(g == 0),
+                stop=(g == PASSES - 1),
+            )
+
+        def saved_values(c):
+            return [gather(SV[c][g], f"sg{c}{g}", s_tab[c], g_list, g) for g in range(PASSES)]
+
+        def gradients_s(c, saved):
+            picked = [gather(GV[c][g], f"gg{c}{g}", g_tab[c], g_list, g) for g in range(PASSES)]
+            quantised = []
+            staged = []
+            for g in range(PASSES):
+                stage = sb.tile([P, 2, P, 2], F32, name=f"stage{c}{g}")
+                for u in range(2):
+                    nc.vector.scalar_tensor_tensor(
+                        stage[:, u],
+                        saved[g][:].rearrange("n (p u e) -> n u p e", u=2, e=2)[:, u],
+                        0.0,
+                        picked[g][:].rearrange("n (p u e) -> n u p e", u=2, e=2)[:, u],
+                        ALU.max,
+                        ALU.mult,
+                    )
+                staged.append(stage)
+            for g in range(PASSES):
+                bank = turn.tile([P, PACK, P], F32, name="bank")
+                for t in range(PACK):
+                    nc.tensor.transpose(bank[:, t, :], staged[g][:, t // 2, :, t % 2], ident[:])
+                g_bf = sb.tile([P, PASS], BF16, name=f"g_bf{c}{g}", align_bytes=64)
+                nc.vector.tensor_tensor(
+                    g_bf[:].rearrange("p (c t) -> p c t", t=PACK),
+                    bank[:].rearrange("p t c -> p c t"),
+                    rb_sb[:, g, :].unsqueeze(1).to_broadcast([P, P, PACK]),
+                    ALU.mult,
+                )
+                codes = sb.tile([P, P], U32, name=f"g_codes{c}{g}", align_bytes=64)
+                scales = sb.tile([P, P], U8, name=f"g_scales{c}{g}", align_bytes=64)
+                nc.vector.quantize_mx(codes[:].bitcast(E5M2), scales[:], g_bf[:])
+                quantised.append((codes, scales))
+            return quantised
+
+        half = N // LIST_ROWS // 2
+
+        features(0)
+        features(1)
+        pre0 = saved_values(0)
+        quantised0 = gradients_s(0, pre0)
+        first = sums.tile([P, 2, P], F32, name="first", tag="w0")
+        for h in range(2):
+            for g in range(PASSES):
+                product(first[:, h, :], h, g, *quantised0[g])
+
+        pre1 = saved_values(1)
+        quantised1 = gradients_s(1, pre1)
+
+        w_first = pre1[0][:, 0 : 2 * P]
+        nc.scalar.copy(w_first, first[:].rearrange("k h n -> k (h n)"))
+        for h in range(2):
+            nc.scalar.activation(placed[h][:].indirect(w_list[:, 0:half]), w_first[:, h * P : (h + 1) * P], COPY)
+
+        second = [sums.tile([P, P], F32, name=f"second{h}", tag=f"w{h}") for h in range(2)]
+        for g in range(PASSES):
+            for h in range(2):
+                product(second[h][:], h, g, *quantised1[g])
+        w_second = [sb.tile([P, P], F32, name=f"w_second{h}") for h in range(2)]
+        nc.vector.tensor_copy(w_second[0][:], second[0][:])
+        nc.scalar.copy(w_second[1][:], second[1][:])
+        nc.vector.tensor_copy(placed[0][:].indirect(w_list[:, half : 2 * half]), w_second[0][:])
+        nc.scalar.activation(placed[1][:].indirect(w_list[:, half : 2 * half]), w_second[1][:], COPY)
+
+        for h in range(2):
+            for c in range(2):
+                cols = slice(c * Q // 2, (c + 1) * Q // 2)
+                result = sb.tile([P, Q // 2], F32, name=f"result{h}{c}")
+                nc.vector.scalar_tensor_tensor(result[:], placed[h][:, cols], STEP, old_sb[h][:, cols], ALU.mult, ALU.add)
+                nc.sync.dma_start(out[rows(h), cols], result[:])

@@ -23,9 +23,9 @@ PASSES = J // PASS
 GROUP = 8
 LIST_ROWS = 16
 STEP = 0.04
-LOADS = "xl x0 x1 ra gl s0 g0 s1 rb g1 wl o0 o1"
-XV = [[512,0],[512,0]]
-SV = [[0,0],[256,0]]
+LOADS = "xl x0 ra x1 gl s0 g0 rb s1 g1 wl o0 o1"
+XV = [[512,0],[256,0]]
+SV = [[0,0],[0,0]]
 GV = [[0,0],[256,0]]
 
 
@@ -64,6 +64,9 @@ def tile_list_moment_centred_saved_placed_kernel(tc, xf, ra, gt, rb, sv, old, of
         for name in LOADS.split():
             nc.sync.dma_start(*loads[name])
 
+        warm = sb.tile([P, 2], F32, name="warm")
+        nc.vector.memset(warm[:, 0:1], 0.0)
+        nc.scalar.activation(warm[:, 1:2], warm[:, 0:1], COPY)
         make_identity(nc, ident[:])
         for h in range(2):
             nc.gpsimd.memset(placed[h][:], 0.0)

@@ -17,16 +17,18 @@ ALU = mybir.AluOpType
 COPY = mybir.ActivationFunctionType.Copy
 
 P = 128
+TILES = 2
 PACK = 4
 PASS = P * PACK
 PASSES = J // PASS
 GROUP = 8
+GROUPS = PASS // GROUP
 LIST_ROWS = 16
 STEP = 0.04
-LOADS = "xl x0 ra x1 gl s0 g0 rb s1 g1 wl o0 o1"
-XV = [[512,0],[256,0]]
-SV = [[0,0],[0,0]]
-GV = [[0,0],[256,0]]
+TURN_BANKS = 6
+
+FEATURE_SLOTS_ON_VECTOR = 512
+GRADIENT_SLOTS_ON_VECTOR = (0, 256)
 
 
 def tile_list_moment_centred_saved_placed_kernel(tc, xf, ra, gt, rb, sv, old, offs, offs2, offs3, out):
@@ -34,108 +36,103 @@ def tile_list_moment_centred_saved_placed_kernel(tc, xf, ra, gt, rb, sv, old, of
     with ExitStack() as ctx:
         lists = ctx.enter_context(tc.tile_pool(name="lists", bufs=1))
         sb = ctx.enter_context(tc.tile_pool(name="sb", bufs=1))
-        turn = ctx.enter_context(tc.psum_pool(name="turn", bufs=6))
+        turn = ctx.enter_context(tc.psum_pool(name="turn", bufs=TURN_BANKS))
         sums = ctx.enter_context(tc.psum_pool(name="sums", bufs=1))
 
         x_list = lists.tile([P, J // LIST_ROWS], U16, name="x_list")
         g_list = lists.tile([P, J // LIST_ROWS], U16, name="g_list")
         w_list = lists.tile([P, N // LIST_ROWS], U16, name="w_list")
-        ra_sb = sb.tile([P, PASSES, PACK], F32, name="ra_sb")
-        rb_sb = sb.tile([P, PASSES, PACK], F32, name="rb_sb")
-        x_tab = [sb.tile([P, T], F32, name=f"x_tab{h}") for h in range(2)]
-        s_tab = [sb.tile([P, V], F32, name=f"s_tab{h}") for h in range(2)]
-        g_tab = [sb.tile([P, V], F32, name=f"g_tab{h}") for h in range(2)]
-        old_sb = [sb.tile([P, Q], F32, name=f"old_sb{h}") for h in range(2)]
-        placed = [sb.tile([P, Q], F32, name=f"placed{h}") for h in range(2)]
+        ra_padded = sb.tile([P, PASSES, 2 * PACK], F32, name="ra_sb")
+        rb_padded = sb.tile([P, PASSES, 2 * PACK], F32, name="rb_sb")
+        ra_sb = ra_padded[:, :, 0:PACK]
+        rb_sb = rb_padded[:, :, 0:PACK]
+        x_tab = [sb.tile([P, T], F32, name=f"x_tab{h}") for h in range(TILES)]
+        s_tab = [sb.tile([P, V], F32, name=f"s_tab{c}") for c in range(TILES)]
+        g_tab = [sb.tile([P, V], F32, name=f"g_tab{c}") for c in range(TILES)]
+        old_sb = [sb.tile([P, Q], F32, name=f"old_sb{h}") for h in range(TILES)]
+        placed = [sb.tile([P, Q], F32, name=f"placed{h}") for h in range(TILES)]
         ident = sb.tile([P, P], F32, name="ident")
 
-        def rows(h):
-            return slice(h * P, (h + 1) * P)
+        def rows(tile_index):
+            return slice(tile_index * P, (tile_index + 1) * P)
 
-        loads = {
-            "xl": (x_list[:], offs), "gl": (g_list[:], offs2), "wl": (w_list[:], offs3),
-            "x0": (x_tab[0][:], xf[rows(0), :]), "x1": (x_tab[1][:], xf[rows(1), :]),
-            "s0": (s_tab[0][:], sv[rows(0), :]), "s1": (s_tab[1][:], sv[rows(1), :]),
-            "g0": (g_tab[0][:], gt[rows(0), :]), "g1": (g_tab[1][:], gt[rows(1), :]),
-            "o0": (old_sb[0][:], old[rows(0), :]), "o1": (old_sb[1][:], old[rows(1), :]),
-            "ra": (ra_sb[:], ra.rearrange("o (g p t) -> p (o g) t", p=P, t=PACK)),
-            "rb": (rb_sb[:], rb.rearrange("o (g p t) -> p (o g) t", p=P, t=PACK)),
-        }
-        for name in LOADS.split():
-            nc.sync.dma_start(*loads[name])
+        def by_slot(weights):
+            return weights.rearrange("o (g p t) -> p (o g) t", p=P, t=PACK)
 
-        warm = sb.tile([P, 2], F32, name="warm")
-        nc.vector.memset(warm[:, 0:1], 0.0)
-        nc.scalar.activation(warm[:, 1:2], warm[:, 0:1], COPY)
+        nc.sync.dma_start(x_list[:], offs)
+        for h in range(TILES):
+            nc.sync.dma_start(x_tab[h][:], xf[rows(h), :])
+        nc.sync.dma_start(ra_sb, by_slot(ra))
+        nc.sync.dma_start(g_list[:], offs2)
+        nc.sync.dma_start(s_tab[0][:], sv[rows(0), :])
+        nc.sync.dma_start(g_tab[0][:], gt[rows(0), :])
+        nc.sync.dma_start(s_tab[1][:], sv[rows(1), :])
+        nc.sync.dma_start(rb_sb, by_slot(rb))
+        nc.sync.dma_start(g_tab[1][:], gt[rows(1), :])
+        nc.sync.dma_start(w_list[:], offs3)
+        for h in range(TILES):
+            nc.sync.dma_start(old_sb[h][:], old[rows(h), :])
+
         make_identity(nc, ident[:])
-        for h in range(2):
+        for h in range(TILES):
             nc.gpsimd.memset(placed[h][:], 0.0)
 
-        def gather(on_vector, name, table, offsets, g):
-            picked = sb.tile([P, PASS], F32, name=name)
-            for lo, hi in ((0, on_vector), (on_vector, PASS)):
-                if hi == lo:
-                    continue
-                src = table[:].indirect(offsets[:, (g * PASS + lo) // LIST_ROWS : (g * PASS + hi) // LIST_ROWS])
-                if hi == on_vector:
-                    nc.vector.tensor_copy(picked[:, lo:hi], src)
-                else:
-                    nc.scalar.activation(picked[:, lo:hi], src, COPY)
+        def gather(name, table, offsets, on_vector):
+            picked = []
+            for g in range(PASSES):
+                columns = sb.tile([P, PASS], F32, name=f"{name}{g}")
+                split = min(max(on_vector - g * PASS, 0), PASS)
+                first_entry = g * PASS
+                if split > 0:
+                    entries = offsets[:, first_entry // LIST_ROWS : (first_entry + split) // LIST_ROWS]
+                    nc.vector.tensor_copy(columns[:, 0:split], table[:].indirect(entries))
+                if split < PASS:
+                    entries = offsets[:, (first_entry + split) // LIST_ROWS : (first_entry + PASS) // LIST_ROWS]
+                    nc.scalar.activation(columns[:, split:PASS], table[:].indirect(entries), COPY)
+                picked.append(columns)
             return picked
 
-        u_codes, u_scales = {}, {}
-        groups = PASS // GROUP
+        def weigh_and_round(rounded, bank, weights):
+            nc.vector.tensor_tensor(
+                rounded.rearrange("p (c t) -> p c t", t=PACK),
+                bank[:].rearrange("p t c -> p c t"),
+                weights.unsqueeze(1).to_broadcast([P, P, PACK]),
+                ALU.mult,
+            )
 
         def features(h):
             u_bf = sb.tile([P, PASSES * PASS], BF16, name=f"u_bf{h}", align_bytes=64)
-            picked = [gather(XV[h][g], f"xg{h}{g}", x_tab[h], x_list, g) for g in range(PASSES)]
+            picked = gather(f"xg{h}", x_tab[h], x_list, FEATURE_SLOTS_ON_VECTOR)
             for g in range(PASSES):
-                xg = picked[g]
-                total = sb.tile([P, groups], F32, name=f"total{h}{g}")
+                total = sb.tile([P, GROUPS], F32, name=f"total{h}{g}")
                 nc.vector.tensor_reduce(
-                    total[:], xg[:].rearrange("k (b i) -> k b i", i=GROUP), mybir.AxisListType.X, ALU.add
+                    total[:], picked[g][:].rearrange("k (b i) -> k b i", i=GROUP), mybir.AxisListType.X, ALU.add
                 )
                 neg_mean = sb.tile([P, P], F32, name=f"neg_mean{h}{g}")
                 nc.vector.tensor_scalar_mul(
                     neg_mean[:].rearrange("k (b e) -> k b e", e=2),
-                    total[:].unsqueeze(2).to_broadcast([P, groups, 2]),
+                    total[:].unsqueeze(2).to_broadcast([P, GROUPS, 2]),
                     -1.0 / GROUP,
                 )
                 bank = turn.tile([P, PACK, P], F32, name="bank")
                 for t in range(PACK):
-                    nc.tensor.matmul(bank[:, t, :], xg[:, t:PASS:PACK], ident[:], start=(t == 0), stop=False, is_transpose=True)
+                    nc.tensor.matmul(
+                        bank[:, t, :], picked[g][:, t:PASS:PACK], ident[:], start=(t == 0), stop=False, is_transpose=True
+                    )
                 for t in range(PACK):
-                    nc.tensor.matmul(bank[:, t, :], neg_mean[:], ident[:], start=False, stop=(t == PACK - 1), is_transpose=True)
-                nc.vector.tensor_tensor(
-                    u_bf[:, g * PASS : (g + 1) * PASS].rearrange("p (c t) -> p c t", t=PACK),
-                    bank[:].rearrange("p t c -> p c t"),
-                    ra_sb[:, g, :].unsqueeze(1).to_broadcast([P, P, PACK]),
-                    ALU.mult,
-                )
+                    nc.tensor.matmul(
+                        bank[:, t, :], neg_mean[:], ident[:], start=False, stop=(t == PACK - 1), is_transpose=True
+                    )
+                weigh_and_round(u_bf[:, g * PASS : (g + 1) * PASS], bank, ra_sb[:, g, :])
             codes = sb.tile([P, PASSES * P], U32, name=f"u_codes{h}", align_bytes=64)
             scales = sb.tile([P, PASSES * P], U8, name=f"u_scales{h}", align_bytes=64)
             nc.vector.quantize_mx(codes[:].bitcast(E4M3), scales[:], u_bf[:])
-            u_codes[h] = codes
-            u_scales[h] = scales
+            return codes, scales
 
-        def product(acc, h, g, codes, scales):
-            nc.tensor.matmul_mx(
-                acc,
-                lhsT=u_codes[h][:, g * P : (g + 1) * P].bitcast(E4M3),
-                lhsT_scale=u_scales[h][:, g * P : (g + 1) * P],
-                rhs=codes[:].bitcast(E5M2),
-                rhs_scale=scales[:],
-                start=(g == 0),
-                stop=(g == PASSES - 1),
-            )
-
-        def saved_values(c):
-            return [gather(SV[c][g], f"sg{c}{g}", s_tab[c], g_list, g) for g in range(PASSES)]
-
-        def gradients_s(c, saved):
-            picked = [gather(GV[c][g], f"gg{c}{g}", g_tab[c], g_list, g) for g in range(PASSES)]
-            quantised = []
-            staged = []
+        def gradients(c):
+            saved = gather(f"sg{c}", s_tab[c], g_list, GRADIENT_SLOTS_ON_VECTOR[c])
+            picked = gather(f"gg{c}", g_tab[c], g_list, GRADIENT_SLOTS_ON_VECTOR[c])
+            gated = []
             for g in range(PASSES):
                 stage = sb.tile([P, 2, P, 2], F32, name=f"stage{c}{g}")
                 for u in range(2):
@@ -147,56 +144,64 @@ def tile_list_moment_centred_saved_placed_kernel(tc, xf, ra, gt, rb, sv, old, of
                         ALU.max,
                         ALU.mult,
                     )
-                staged.append(stage)
+                gated.append(stage)
+            quantised = []
             for g in range(PASSES):
                 bank = turn.tile([P, PACK, P], F32, name="bank")
                 for t in range(PACK):
-                    nc.tensor.transpose(bank[:, t, :], staged[g][:, t // 2, :, t % 2], ident[:])
+                    nc.tensor.transpose(bank[:, t, :], gated[g][:, t // 2, :, t % 2], ident[:])
                 g_bf = sb.tile([P, PASS], BF16, name=f"g_bf{c}{g}", align_bytes=64)
-                nc.vector.tensor_tensor(
-                    g_bf[:].rearrange("p (c t) -> p c t", t=PACK),
-                    bank[:].rearrange("p t c -> p c t"),
-                    rb_sb[:, g, :].unsqueeze(1).to_broadcast([P, P, PACK]),
-                    ALU.mult,
-                )
+                weigh_and_round(g_bf[:], bank, rb_sb[:, g, :])
                 codes = sb.tile([P, P], U32, name=f"g_codes{c}{g}", align_bytes=64)
                 scales = sb.tile([P, P], U8, name=f"g_scales{c}{g}", align_bytes=64)
                 nc.vector.quantize_mx(codes[:].bitcast(E5M2), scales[:], g_bf[:])
                 quantised.append((codes, scales))
-            return quantised
+            return quantised, saved
 
-        half = N // LIST_ROWS // 2
+        u_quantised = [features(h) for h in range(TILES)]
 
-        features(0)
-        features(1)
-        pre0 = saved_values(0)
-        quantised0 = gradients_s(0, pre0)
-        first = sums.tile([P, 2, P], F32, name="first", tag="w0")
-        for h in range(2):
+        def product(acc, h, g, g_quantised):
+            u_codes, u_scales = u_quantised[h]
+            g_codes, g_scales = g_quantised[g]
+            nc.tensor.matmul_mx(
+                acc,
+                lhsT=u_codes[:, g * P : (g + 1) * P].bitcast(E4M3),
+                lhsT_scale=u_scales[:, g * P : (g + 1) * P],
+                rhs=g_codes[:].bitcast(E5M2),
+                rhs_scale=g_scales[:],
+                start=(g == 0),
+                stop=(g == PASSES - 1),
+            )
+
+        def places(c):
+            return w_list[:, c * P // LIST_ROWS : (c + 1) * P // LIST_ROWS]
+
+        early_quantised = gradients(0)[0]
+        early = sums.tile([P, TILES, P], F32, name="first", tag="w0")
+        for h in range(TILES):
             for g in range(PASSES):
-                product(first[:, h, :], h, g, *quantised0[g])
+                product(early[:, h, :], h, g, early_quantised)
 
-        pre1 = saved_values(1)
-        quantised1 = gradients_s(1, pre1)
+        late_quantised, late_saved = gradients(1)
 
-        w_first = pre1[0][:, 0 : 2 * P]
-        nc.scalar.copy(w_first, first[:].rearrange("k h n -> k (h n)"))
-        for h in range(2):
-            nc.scalar.activation(placed[h][:].indirect(w_list[:, 0:half]), w_first[:, h * P : (h + 1) * P], COPY)
+        w_early = late_saved[0][:, 0 : TILES * P]
+        nc.scalar.copy(w_early, early[:].rearrange("k h n -> k (h n)"))
+        for h in range(TILES):
+            nc.scalar.activation(placed[h][:].indirect(places(0)), w_early[:, h * P : (h + 1) * P], COPY)
 
-        second = [sums.tile([P, P], F32, name=f"second{h}", tag=f"w{h}") for h in range(2)]
+        late = [sums.tile([P, P], F32, name=f"second{h}", tag=f"w{h}") for h in range(TILES)]
         for g in range(PASSES):
-            for h in range(2):
-                product(second[h][:], h, g, *quantised1[g])
-        w_second = [sb.tile([P, P], F32, name=f"w_second{h}") for h in range(2)]
-        nc.vector.tensor_copy(w_second[0][:], second[0][:])
-        nc.scalar.copy(w_second[1][:], second[1][:])
-        nc.vector.tensor_copy(placed[0][:].indirect(w_list[:, half : 2 * half]), w_second[0][:])
-        nc.scalar.activation(placed[1][:].indirect(w_list[:, half : 2 * half]), w_second[1][:], COPY)
+            for h in range(TILES):
+                product(late[h][:], h, g, late_quantised)
+        w_late = [sb.tile([P, P], F32, name=f"w_second{h}") for h in range(TILES)]
+        nc.vector.tensor_copy(w_late[0][:], late[0][:])
+        nc.scalar.copy(w_late[1][:], late[1][:])
+        nc.vector.tensor_copy(placed[0][:].indirect(places(1)), w_late[0][:])
+        nc.scalar.activation(placed[1][:].indirect(places(1)), w_late[1][:], COPY)
 
-        for h in range(2):
-            for c in range(2):
-                cols = slice(c * Q // 2, (c + 1) * Q // 2)
-                result = sb.tile([P, Q // 2], F32, name=f"result{h}{c}")
+        for h in range(TILES):
+            for half in range(2):
+                cols = slice(half * Q // 2, (half + 1) * Q // 2)
+                result = sb.tile([P, Q // 2], F32, name=f"result{h}{half}")
                 nc.vector.scalar_tensor_tensor(result[:], placed[h][:, cols], STEP, old_sb[h][:, cols], ALU.mult, ALU.add)
                 nc.sync.dma_start(out[rows(h), cols], result[:])

from contextlib import ExitStack

import concourse.mybir as mybir
from concourse.masks import make_identity

K, J, N, T, V, Q = 256, 1024, 256, 2048, 2048, 1024
FLOPS = 2 * K * N * J

F32 = mybir.dt.float32
BF16 = mybir.dt.bfloat16
U32 = mybir.dt.uint32
U16 = mybir.dt.uint16
U8 = mybir.dt.uint8
E4M3 = mybir.dt.float8_e4m3fn_x4
E5M2 = mybir.dt.float8_e5m2_x4
ALU = mybir.AluOpType
COPY = mybir.ActivationFunctionType.Copy

P = 128
TILES = 2
PACK = 4
PASS = P * PACK
PASSES = J // PASS
GROUP = 8
GROUPS = PASS // GROUP
LIST_ROWS = 16
STEP = 0.04
TURN_BANKS = 6

FEATURE_SLOTS_ON_VECTOR = 512
GRADIENT_SLOTS_ON_VECTOR = (0, 256)


def tile_list_moment_centred_saved_placed_kernel(tc, xf, ra, gt, rb, sv, old, offs, offs2, offs3, out):
    nc = tc.nc
    with ExitStack() as ctx:
        lists = ctx.enter_context(tc.tile_pool(name="lists", bufs=1))
        sb = ctx.enter_context(tc.tile_pool(name="sb", bufs=1))
        turn = ctx.enter_context(tc.psum_pool(name="turn", bufs=TURN_BANKS))
        sums = ctx.enter_context(tc.psum_pool(name="sums", bufs=1))

        x_list = lists.tile([P, J // LIST_ROWS], U16, name="x_list")
        g_list = lists.tile([P, J // LIST_ROWS], U16, name="g_list")
        w_list = lists.tile([P, N // LIST_ROWS], U16, name="w_list")
        ra_padded = sb.tile([P, PASSES, 2 * PACK], F32, name="ra_sb")
        rb_padded = sb.tile([P, PASSES, 2 * PACK], F32, name="rb_sb")
        ra_sb = ra_padded[:, :, 0:PACK]
        rb_sb = rb_padded[:, :, 0:PACK]
        x_tab = [sb.tile([P, T], F32, name=f"x_tab{h}") for h in range(TILES)]
        s_tab = [sb.tile([P, V], F32, name=f"s_tab{c}") for c in range(TILES)]
        g_tab = [sb.tile([P, V], F32, name=f"g_tab{c}") for c in range(TILES)]
        old_sb = [sb.tile([P, Q], F32, name=f"old_sb{h}") for h in range(TILES)]
        placed = [sb.tile([P, Q], F32, name=f"placed{h}") for h in range(TILES)]
        ident = sb.tile([P, P], F32, name="ident")

        def rows(tile_index):
            return slice(tile_index * P, (tile_index + 1) * P)

        def by_slot(weights):
            return weights.rearrange("o (g p t) -> p (o g) t", p=P, t=PACK)

        nc.sync.dma_start(x_list[:], offs)
        for h in range(TILES):
            nc.sync.dma_start(x_tab[h][:], xf[rows(h), :])
        nc.sync.dma_start(ra_sb, by_slot(ra))
        nc.sync.dma_start(g_list[:], offs2)
        nc.sync.dma_start(s_tab[0][:], sv[rows(0), :])
        nc.sync.dma_start(g_tab[0][:], gt[rows(0), :])
        nc.sync.dma_start(s_tab[1][:], sv[rows(1), :])
        nc.sync.dma_start(rb_sb, by_slot(rb))
        nc.sync.dma_start(g_tab[1][:], gt[rows(1), :])
        nc.sync.dma_start(w_list[:], offs3)
        for h in range(TILES):
            nc.sync.dma_start(old_sb[h][:], old[rows(h), :])

        make_identity(nc, ident[:])
        for h in range(TILES):
            nc.gpsimd.memset(placed[h][:], 0.0)

        def gather(name, table, offsets, on_vector):
            picked = []
            for g in range(PASSES):
                columns = sb.tile([P, PASS], F32, name=f"{name}{g}")
                split = min(max(on_vector - g * PASS, 0), PASS)
                first_entry = g * PASS
                if split > 0:
                    entries = offsets[:, first_entry // LIST_ROWS : (first_entry + split) // LIST_ROWS]
                    nc.vector.tensor_copy(columns[:, 0:split], table[:].indirect(entries))
                if split < PASS:
                    entries = offsets[:, (first_entry + split) // LIST_ROWS : (first_entry + PASS) // LIST_ROWS]
                    nc.scalar.activation(columns[:, split:PASS], table[:].indirect(entries), COPY)
                picked.append(columns)
            return picked

        def weigh_and_round(rounded, bank, weights):
            nc.vector.tensor_tensor(
                rounded.rearrange("p (c t) -> p c t", t=PACK),
                bank[:].rearrange("p t c -> p c t"),
                weights.unsqueeze(1).to_broadcast([P, P, PACK]),
                ALU.mult,
            )

        def features(h):
            u_bf = sb.tile([P, PASSES * PASS], BF16, name=f"u_bf{h}", align_bytes=64)
            picked = gather(f"xg{h}", x_tab[h], x_list, FEATURE_SLOTS_ON_VECTOR)
            for g in range(PASSES):
                total = sb.tile([P, GROUPS], F32, name=f"total{h}{g}")
                nc.vector.tensor_reduce(
                    total[:], picked[g][:].rearrange("k (b i) -> k b i", i=GROUP), mybir.AxisListType.X, ALU.add
                )
                neg_mean = sb.tile([P, P], F32, name=f"neg_mean{h}{g}")
                nc.vector.tensor_scalar_mul(
                    neg_mean[:].rearrange("k (b e) -> k b e", e=2),
                    total[:].unsqueeze(2).to_broadcast([P, GROUPS, 2]),
                    -1.0 / GROUP,
                )
                bank = turn.tile([P, PACK, P], F32, name="bank")
                for t in range(PACK):
                    nc.tensor.matmul(
                        bank[:, t, :], picked[g][:, t:PASS:PACK], ident[:], start=(t == 0), stop=False, is_transpose=True
                    )
                for t in range(PACK):
                    nc.tensor.matmul(
                        bank[:, t, :], neg_mean[:], ident[:], start=False, stop=(t == PACK - 1), is_transpose=True
                    )
                weigh_and_round(u_bf[:, g * PASS : (g + 1) * PASS], bank, ra_sb[:, g, :])
            codes = sb.tile([P, PASSES * P], U32, name=f"u_codes{h}", align_bytes=64)
            scales = sb.tile([P, PASSES * P], U8, name=f"u_scales{h}", align_bytes=64)
            nc.vector.quantize_mx(codes[:].bitcast(E4M3), scales[:], u_bf[:])
            return codes, scales

        def gradients(c):
            saved = gather(f"sg{c}", s_tab[c], g_list, GRADIENT_SLOTS_ON_VECTOR[c])
            picked = gather(f"gg{c}", g_tab[c], g_list, GRADIENT_SLOTS_ON_VECTOR[c])
            gated = []
            for g in range(PASSES):
                stage = sb.tile([P, 2, P, 2], F32, name=f"stage{c}{g}")
                for u in range(2):
                    nc.vector.scalar_tensor_tensor(
                        stage[:, u],
                        saved[g][:].rearrange("n (p u e) -> n u p e", u=2, e=2)[:, u],
                        0.0,
                        picked[g][:].rearrange("n (p u e) -> n u p e", u=2, e=2)[:, u],
                        ALU.max,
                        ALU.mult,
                    )
                gated.append(stage)
            quantised = []
            for g in range(PASSES):
                bank = turn.tile([P, PACK, P], F32, name="bank")
                for t in range(PACK):
                    nc.tensor.transpose(bank[:, t, :], gated[g][:, t // 2, :, t % 2], ident[:])
                g_bf = sb.tile([P, PASS], BF16, name=f"g_bf{c}{g}", align_bytes=64)
                weigh_and_round(g_bf[:], bank, rb_sb[:, g, :])
                codes = sb.tile([P, P], U32, name=f"g_codes{c}{g}", align_bytes=64)
                scales = sb.tile([P, P], U8, name=f"g_scales{c}{g}", align_bytes=64)
                nc.vector.quantize_mx(codes[:].bitcast(E5M2), scales[:], g_bf[:])
                quantised.append((codes, scales))
            return quantised, saved

        u_quantised = [features(h) for h in range(TILES)]

        def product(acc, h, g, g_quantised):
            u_codes, u_scales = u_quantised[h]
            g_codes, g_scales = g_quantised[g]
            nc.tensor.matmul_mx(
                acc,
                lhsT=u_codes[:, g * P : (g + 1) * P].bitcast(E4M3),
                lhsT_scale=u_scales[:, g * P : (g + 1) * P],
                rhs=g_codes[:].bitcast(E5M2),
                rhs_scale=g_scales[:],
                start=(g == 0),
                stop=(g == PASSES - 1),
            )

        def places(c):
            return w_list[:, c * P // LIST_ROWS : (c + 1) * P // LIST_ROWS]

        early_quantised = gradients(0)[0]
        early = sums.tile([P, TILES, P], F32, name="first", tag="w0")
        for h in range(TILES):
            for g in range(PASSES):
                product(early[:, h, :], h, g, early_quantised)

        late_quantised, late_saved = gradients(1)

        w_early = late_saved[0][:, 0 : TILES * P]
        nc.scalar.copy(w_early, early[:].rearrange("k h n -> k (h n)"))
        for h in range(TILES):
            nc.scalar.activation(placed[h][:].indirect(places(0)), w_early[:, h * P : (h + 1) * P], COPY)

        late = [sums.tile([P, P], F32, name=f"second{h}", tag=f"w{h}") for h in range(TILES)]
        for g in range(PASSES):
            for h in range(TILES):
                product(late[h][:], h, g, late_quantised)
        w_late = [sb.tile([P, P], F32, name=f"w_second{h}") for h in range(TILES)]
        nc.vector.tensor_copy(w_late[0][:], late[0][:])
        nc.scalar.copy(w_late[1][:], late[1][:])
        nc.vector.tensor_copy(placed[0][:].indirect(places(1)), w_late[0][:])
        nc.scalar.activation(placed[1][:].indirect(places(1)), w_late[1][:], COPY)

        for h in range(TILES):
            for half in range(2):
                cols = slice(half * Q // 2, (half + 1) * Q // 2)
                result = sb.tile([P, Q // 2], F32, name=f"result{h}{half}")
                nc.vector.scalar_tensor_tensor(result[:], placed[h][:, cols], STEP, old_sb[h][:, cols], ALU.mult, ALU.add)
                nc.sync.dma_start(out[rows(h), cols], result[:])
